import numpy as np
import ml_dtypes


def mxq(x, axis, fmt="e4m3"):
    dtype, down = {"e4m3": (ml_dtypes.float8_e4m3fn, 7), "e5m2": (ml_dtypes.float8_e5m2, 14)}[fmt]
    v = np.moveaxis(np.asarray(x, np.float32).astype(ml_dtypes.bfloat16).astype(np.float64), axis, -1)
    blocks = v.reshape(v.shape[:-1] + (-1, 32))
    amax = np.abs(blocks).max(-1, keepdims=True)
    byte = np.maximum(np.where(amax > 0, np.frexp(amax)[1] - 1 + 127, 0) - down, 1)
    scale = np.exp2(byte - 127.0)
    codes = (blocks / scale).astype(np.float32).astype(dtype).astype(np.float64)
    return np.moveaxis((codes * scale).reshape(v.shape), -1, axis)


WIDE = False


def mx_kscale(k):
    if not WIDE:
        return np.ones(k)
    levels = np.array([10, -10, 5, -5, 0])
    if k % 512:
        return np.exp2(np.random.permutation(np.resize(levels, k // 32))).repeat(32)
    a = np.empty((k // 512, 16))
    for p in range(k // 512):
        a[p, :8] = np.random.permutation(np.resize(levels, 8))
        for g in range(8):
            far = levels[np.abs(levels - a[p, g]) >= 10]
            a[p, g + 8] = far[np.random.randint(len(far))]
    return np.exp2(a.ravel()).repeat(32)


def f64(x):
    return np.asarray(x).astype(np.float64)


def striped(idx):
    return np.tile(idx.reshape(-1, 16).T, (8, 1)).astype(np.uint16)


def unstriped(offs):
    return offs[:16].T.reshape(-1).astype(np.int64)


def pack_weight(w):
    k, n = w.shape
    w = f64(np.asarray(w, np.float32).astype(ml_dtypes.bfloat16)).reshape(k // 32, 32, n)
    amax = np.abs(w).max(1)
    byte = np.clip(np.where(amax > 0, np.frexp(amax)[1] - 1 + 127 - 7, 1), 1, 254)
    scaled = (w * np.exp2(127.0 - byte)[:, None, :]).reshape(k, n).astype(np.float32)
    words = np.ascontiguousarray(scaled.reshape(k // 512, 128, 4, n).transpose(0, 1, 3, 2)).astype(ml_dtypes.float8_e4m3fn).view(np.uint8)
    return words, np.ascontiguousarray(byte.astype(np.uint8).reshape(k // 512, 16, n))


def unpack_weight(words, scales):
    g, p, n, _ = words.shape
    vals = np.ascontiguousarray(words).view(ml_dtypes.float8_e4m3fn).astype(np.float64) * np.repeat(np.exp2(scales.astype(np.float64) - 127.0), 8, axis=1)[..., None]
    return vals.transpose(0, 1, 3, 2).reshape(g * 512, n)


def silu(v):
    return v / (1.0 + np.exp(-np.maximum(v, -700.0)))


K, T, E, C, N = 1536, 1024, 8, 256, 128


def by_expert(wq, xq):
    return np.concatenate([wq[e].T @ xq[:, e * C:(e + 1) * C] for e in range(E)], axis=1)


def setup_inputs():
    n = np.random.standard_normal
    s = mx_kscale(K)[:, None]
    first = np.random.permutation(np.repeat(np.arange(E), T // E))
    second = (first + 1 + np.random.permutation(np.repeat(np.arange(E - 1), -(-T // (E - 1)))[:T])) % E
    while np.bincount(second, minlength=E).max() != T // E:
        load = np.bincount(second, minlength=E); hi, lo = int(load.argmax()), int(load.argmin())
        t = np.flatnonzero((second == hi) & (first != lo))[0]; second[t] = lo
    slot_token = np.empty(E * C, np.int64); pos = np.empty((2, T), np.int64); fill = np.zeros(E, np.int64)
    place = np.stack([np.random.permutation(C) for _ in range(E)])
    for r, deal in enumerate((first, second)):
        for t in np.random.permutation(T):
            e = deal[t]; j = e * C + place[e, fill[e]]; fill[e] += 1; slot_token[j] = t; pos[r, t] = j
    g = np.random.uniform(0.2, 0.8, T)
    packed = [pack_weight(m) for m in n((E, K, N)) / np.sqrt(K) / s[None]]
    return {
        "xT": (n((K, T)) * s).astype(np.float32),
        "w_words": np.stack([m[0] for m in packed]),
        "w_scales": np.stack([m[1] for m in packed]),
        "b": (0.3 * n((N, E))).astype(np.float32),
        "gate": np.stack([np.tile(g, (N, 1)), np.tile(1.0 - g, (N, 1))]).astype(np.float32),
        "offs": striped(slot_token),
        "pos1": striped(pos[0]),
        "pos2": striped(pos[1]),
    }


def reference(xT, w_words, w_scales, b, gate, offs, pos1, pos2):
    idx = unstriped(offs)
    xq = mxq(f64(xT)[:, idx], 0, "e4m3")
    w = np.stack([unpack_weight(w_words[e], w_scales[e]) for e in range(E)])
    y = by_expert(w, xq)
    y = silu(y + np.repeat(f64(b), C, axis=1))
    return f64(gate[0]) * y[:, unstriped(pos1)] + f64(gate[1]) * y[:, unstriped(pos2)]

@@ -1,0 +1,157 @@
+from contextlib import ExitStack
+
+import concourse.mybir as mybir
+
+K, T, E, C, N = 1536, 1024, 8, 256, 128
+FLOPS = 2 * K * E * C * N
+
+F32 = mybir.dt.float32
+BF16 = mybir.dt.bfloat16
+I32 = mybir.dt.int32
+U32 = mybir.dt.uint32
+U16 = mybir.dt.uint16
+U8 = mybir.dt.uint8
+FP8X4 = mybir.dt.float8_e4m3fn_x4
+MULT = mybir.AluOpType.mult
+ADD = mybir.AluOpType.add
+SILU = mybir.ActivationFunctionType.Silu
+
+P = 128
+PASSES = K // 512
+S = E * C
+
+CHUNKS = (
+    ((0, 512, 336), (512, 256, 160), (768, 256, 160)),
+    ((0, 512, 128), (512, 512, 256)),
+    ((0, 512, 0), (512, 512, 0)),
+)
+PIECES = ((0, 768), (768, 768), (1536, 512))
+LAST_PIECES = ((0, 768), (768, 768), (1536, 384), (1920, 128))
+
+
+def tile_routed_moe_kernel(tc, xT, w_words, w_scales, b, gate, offs, pos1, pos2, out):
+    nc = tc.nc
+    with ExitStack() as ctx:
+        lists = ctx.enter_context(tc.tile_pool(name="lists", bufs=1))
+        keep = ctx.enter_context(tc.tile_pool(name="keep", bufs=1))
+        psum = ctx.enter_context(tc.psum_pool(name="psum", bufs=1))
+
+        offs_t = lists.tile([P, S // 16], U16, name="offs_t")
+        pos1_t = lists.tile([P, T // 16], U16, name="pos1_t")
+        pos2_t = lists.tile([P, T // 16], U16, name="pos2_t")
+
+        raws = {}
+        for a in range(PASSES):
+            for i, (t0, n, v) in enumerate(CHUNKS[a]):
+                raw = keep.tile([P, 4, n], F32, name=f"raw{a}_{i}")
+                raws[a, i] = raw
+                nc.sync.dma_start(raw[:], xT[512 * a : 512 * (a + 1), t0 : t0 + n].rearrange("(p t) n -> p t n", t=4))
+                if a == 0 and i == 0:
+                    nc.sync.dma_start(offs_t[:], offs)
+
+        wsc = keep.tile([P, E * PASSES * N // 4], I32, name="wsc", align_bytes=64)
+        nc.vector.memset(wsc[:], 0)
+        plane = keep.tile([P, T], U8, name="plane", align_bytes=64)
+        nc.gpsimd.memset(plane[:], 0)
+        one = keep.tile([P, 1], F32, name="one")
+        nc.vector.memset(one[:], 0.0)
+        warm = keep.tile([P, 1], F32, name="warm")
+        nc.scalar.activation(warm[:], one[:], SILU)
+
+        w = keep.tile([P, E * PASSES * N], I32, name="w", align_bytes=64)
+        w_hbm = w_words.rearrange("e a p n r -> e a p (n r)").bitcast(I32).rearrange("e a p n -> p (e a) n")
+        half = E * PASSES // 2
+        for h in range(2):
+            nc.sync.dma_start(
+                w[:, h * half * N : (h + 1) * half * N].rearrange("p (g n) -> p g n", n=N),
+                w_hbm[:, h * half : (h + 1) * half, :],
+            )
+        for q in range(4):
+            nc.sync.dma_start(
+                wsc[32 * q : 32 * q + 4, :].rearrange("r (g n) -> r g n", n=N // 4),
+                w_scales.bitcast(I32)[:, :, 4 * q : 4 * q + 4, :].rearrange("e a r n -> r (e a) n"),
+            )
+        bias = keep.tile([P, E], F32, name="bias")
+        nc.sync.dma_start(bias[:], b)
+        nc.sync.dma_start(pos1_t[:], pos1)
+        gates = []
+        for r in range(2):
+            g = keep.tile([P, T], F32, name=f"gate{r}")
+            gates.append(g)
+            nc.sync.dma_start(g[:], gate[r])
+            if r == 0:
+                nc.sync.dma_start(pos2_t[:], pos2)
+
+        gbytes = keep.tile([P, S], U8, name="gbytes", align_bytes=64)
+        words = []
+        gwords = []
+        for a in range(PASSES):
+            wt = keep.tile([P, T], U32, name=f"words{a}", align_bytes=64)
+            words.append(wt)
+            gt = keep.tile([P, S], U32, name=f"gwords{a}", align_bytes=64)
+            gwords.append(gt)
+
+        def gather(dst, src, lo, n):
+            nc.vector.tensor_copy(dst[:, lo : lo + n], src[:].indirect(offs_t[:, lo // 16 : (lo + n) // 16]))
+
+        def cast(engine_copy, grouped, raw, lo, hi):
+            engine_copy(
+                grouped[:, 4 * lo : 4 * hi].rearrange("p (c i t) -> p c t i", i=4, t=4),
+                raw[:, :, lo:hi].rearrange("p t (c i) -> p c t i", i=4),
+            )
+
+        for a in range(PASSES):
+            for i, (t0, n, v) in enumerate(CHUNKS[a]):
+                grouped = keep.tile([P, 4 * n], BF16, name=f"grouped{a}_{i}", align_bytes=64)
+                if v < n:
+                    cast(nc.scalar.copy, grouped, raws[a, i], v, n)
+                if v > 0:
+                    cast(nc.vector.tensor_copy, grouped, raws[a, i], 0, v)
+                nc.vector.quantize_mx(
+                    out=words[a][:, t0 : t0 + n].bitcast(FP8X4),
+                    scales=plane[4 * a : P, t0 : t0 + n],
+                    in_=grouped[:],
+                )
+            if a < PASSES - 1:
+                for lo, n in PIECES:
+                    gather(gwords[a], words[a], lo, n)
+        for lo, n in PIECES:
+            gather(gbytes, plane, lo, n)
+
+        y = keep.tile([P, S], F32, name="y")
+
+        def mm(acc, e, lo, n, passes):
+            for a in passes:
+                g = e * PASSES + a
+                nc.tensor.matmul_mx(
+                    out=acc,
+                    lhsT=w[:, g * N : (g + 1) * N].bitcast(FP8X4),
+                    lhsT_scale=wsc[:, g * N // 4 : (g + 1) * N // 4].bitcast(U8),
+                    rhs=gwords[a][:, lo : lo + n].bitcast(FP8X4),
+                    rhs_scale=gbytes[4 * a : P, lo : lo + n],
+                    start=(a == 0),
+                    stop=(a == PASSES - 1),
+                )
+
+        a = PASSES - 1
+        for lo, n in LAST_PIECES:
+            gather(gwords[a], words[a], lo, n)
+            s = lo
+            while s < lo + n:
+                e = s // C
+                m = min(C * (e + 1), lo + n) - s
+                acc = psum.tile([P, 512], F32, name=f"acc{(s // 128) % 8}")
+                mm(acc[:, 0:m], e, s, m, range(PASSES))
+                nc.scalar.activation(y[:, s : s + m], acc[:, 0:m], SILU, bias=bias[:, e : e + 1])
+                s += m
+
+        m1 = keep.tile([P, T], F32, name="m1")
+        m2 = keep.tile([P, T], F32, name="m2")
+        res = keep.tile([P, T], F32, name="res")
+        H = T // 2
+        nc.vector.tensor_tensor(m1[:], y[:].indirect(pos1_t[:]), gates[0][:], MULT)
+        for h in range(2):
+            cols = slice(h * H, (h + 1) * H)
+            nc.vector.tensor_tensor(m2[:, cols], y[:].indirect(pos2_t[:, h * H // 16 : (h + 1) * H // 16]), gates[1][:, cols], MULT)
+            nc.vector.tensor_tensor(res[:, cols], m1[:, cols], m2[:, cols], ADD)
+            nc.sync.dma_start(out[:, cols], res[:, cols])

@@ -1,6 +1,7 @@
 from contextlib import ExitStack
 
 import concourse.mybir as mybir
+from concourse.masks import make_identity
 
 K, T, E, C, N = 1536, 1024, 8, 256, 128
 FLOPS = 2 * K * E * C * N
@@ -22,10 +23,11 @@ S = E * C
 
 CHUNKS = (
     ((0, 512, 336), (512, 256, 160), (768, 256, 160)),
-    ((0, 512, 128), (512, 512, 256)),
+    ((0, 512, 0), (512, 512, 128)),
     ((0, 512, 0), (512, 512, 0)),
 )
 PIECES = ((0, 768), (768, 768), (1536, 512))
+ROWS = (4, 8, 0)
 LAST_PIECES = ((0, 768), (768, 768), (1536, 384), (1920, 128))
 
 
@@ -53,6 +55,8 @@ def tile_routed_moe_kernel(tc, xT, w_words, w_scales, b, gate, offs, pos1, pos2,
         nc.vector.memset(wsc[:], 0)
         plane = keep.tile([P, T], U8, name="plane", align_bytes=64)
         nc.gpsimd.memset(plane[:], 0)
+        ident = keep.tile([P, P], F32, name="ident")
+        make_identity(nc, ident[:])
         one = keep.tile([P, 1], F32, name="one")
         nc.vector.memset(one[:], 0.0)
         warm = keep.tile([P, 1], F32, name="warm")
@@ -100,18 +104,27 @@ def tile_routed_moe_kernel(tc, xT, w_words, w_scales, b, gate, offs, pos1, pos2,
                 raw[:, :, lo:hi].rearrange("p t (c i) -> p c t i", i=4),
             )
 
+        def quantise(a, t0, n, grouped):
+            nc.vector.quantize_mx(
+                out=words[a][:, t0 : t0 + n].bitcast(FP8X4),
+                scales=plane[ROWS[a] : P, t0 : t0 + n],
+                in_=grouped[:],
+            )
+
         for a in range(PASSES):
-            for i, (t0, n, v) in enumerate(CHUNKS[a]):
-                grouped = keep.tile([P, 4 * n], BF16, name=f"grouped{a}_{i}", align_bytes=64)
-                if v < n:
-                    cast(nc.scalar.copy, grouped, raws[a, i], v, n)
-                if v > 0:
-                    cast(nc.vector.tensor_copy, grouped, raws[a, i], 0, v)
-                nc.vector.quantize_mx(
-                    out=words[a][:, t0 : t0 + n].bitcast(FP8X4),
-                    scales=plane[4 * a : P, t0 : t0 + n],
-                    in_=grouped[:],
-                )
+            if a < PASSES - 1:
+                for i, (t0, n, v) in enumerate(CHUNKS[a]):
+                    grouped = keep.tile([P, 4 * n], BF16, name=f"grouped{a}_{i}", align_bytes=64)
+                    if v < n:
+                        cast(nc.scalar.copy, grouped[:], raws[a, i], v, n)
+                    if v > 0:
+                        cast(nc.vector.tensor_copy, grouped[:], raws[a, i], 0, v)
+                    quantise(a, t0, n, grouped)
+            else:
+                grouped = keep.tile([P, 4 * T], BF16, name="grouped_last", align_bytes=64)
+                for i, (t0, n, v) in enumerate(CHUNKS[a]):
+                    cast(nc.scalar.copy, grouped[:, 4 * t0 : 4 * (t0 + n)], raws[a, i], 0, n)
+                quantise(a, 0, T, grouped)
             if a < PASSES - 1:
                 for lo, n in PIECES:
                     gather(gwords[a], words[a], lo, n)
@@ -128,30 +141,50 @@ def tile_routed_moe_kernel(tc, xT, w_words, w_scales, b, gate, offs, pos1, pos2,
                     lhsT=w[:, g * N : (g + 1) * N].bitcast(FP8X4),
                     lhsT_scale=wsc[:, g * N // 4 : (g + 1) * N // 4].bitcast(U8),
                     rhs=gwords[a][:, lo : lo + n].bitcast(FP8X4),
-                    rhs_scale=gbytes[4 * a : P, lo : lo + n],
+                    rhs_scale=gbytes[ROWS[a] : P, lo : lo + n],
                     start=(a == 0),
                     stop=(a == PASSES - 1),
                 )
 
-        a = PASSES - 1
+        groups = [(e, C * e, C) for e in range(E - 1)] + [(E - 1, S - C, N), (E - 1, S - N, N)]
+        accs = {}
+        last = PASSES - 1
+
+        def open_group(g):
+            e, s, m = g
+            acc = psum.tile([P, 512], F32, name=f"acc{groups.index(g) % 7}")
+            accs[s] = acc
+            mm(acc[:, 0:m], e, s, m, range(last))
+
+        def close_group(g):
+            e, s, m = g
+            mm(accs[s][:, 0:m], e, s, m, (last,))
+            nc.scalar.activation(y[:, s : s + m], accs[s][:, 0:m], SILU, bias=bias[:, e : e + 1])
+
+        for g in groups[:7]:
+            open_group(g)
         for lo, n in LAST_PIECES:
-            gather(gwords[a], words[a], lo, n)
-            s = lo
-            while s < lo + n:
-                e = s // C
-                m = min(C * (e + 1), lo + n) - s
-                acc = psum.tile([P, 512], F32, name=f"acc{(s // 128) % 8}")
-                mm(acc[:, 0:m], e, s, m, range(PASSES))
-                nc.scalar.activation(y[:, s : s + m], acc[:, 0:m], SILU, bias=bias[:, e : e + 1])
-                s += m
+            gather(gwords[last], words[last], lo, n)
+            for g in groups:
+                if lo <= g[1] < lo + n:
+                    close_group(g)
+            if lo == 0:
+                for g in groups[7:]:
+                    open_group(g)
 
         m1 = keep.tile([P, T], F32, name="m1")
         m2 = keep.tile([P, T], F32, name="m2")
         res = keep.tile([P, T], F32, name="res")
-        H = T // 2
         nc.vector.tensor_tensor(m1[:], y[:].indirect(pos1_t[:]), gates[0][:], MULT)
-        for h in range(2):
-            cols = slice(h * H, (h + 1) * H)
-            nc.vector.tensor_tensor(m2[:, cols], y[:].indirect(pos2_t[:, h * H // 16 : (h + 1) * H // 16]), gates[1][:, cols], MULT)
-            nc.vector.tensor_tensor(res[:, cols], m1[:, cols], m2[:, cols], ADD)
-            nc.sync.dma_start(out[:, cols], res[:, cols])
+        R = 384
+        for lo, hi in ((0, R), (R, T)):
+            nc.vector.tensor_tensor(m2[:, lo:hi], y[:].indirect(pos2_t[:, lo // 16 : hi // 16]), gates[1][:, lo:hi], MULT)
+            if lo == 0:
+                total = psum.tile([P, 512], F32, name="total")
+                nc.tensor.matmul(total[:, 0:R], ident[:], m1[:, 0:R], start=True, stop=False)
+                nc.tensor.matmul(total[:, 0:R], ident[:], m2[:, 0:R], start=False, stop=True)
+                nc.scalar.copy(res[:, 0:R], total[:, 0:R])
+                nc.sync.dma_start(out[:, 0:R], res[:, 0:R])
+        for lo, hi in ((R, 768), (768, T)):
+            nc.vector.tensor_tensor(res[:, lo:hi], m1[:, lo:hi], m2[:, lo:hi], ADD)
+            nc.sync.dma_start(out[:, lo:hi], res[:, lo:hi])

@@ -21,11 +21,9 @@ P = 128
 PASSES = K // 512
 S = E * C
 
-CHUNKS = (
-    ((0, 512, 336), (512, 256, 160), (768, 256, 160)),
-    ((0, 512, 0), (512, 512, 128)),
-    ((0, 512, 0), (512, 512, 0)),
-)
+LOADS = ((512, 256, 256), (256, 256, 256, 256), (512, 512))
+VECTOR_CASTS = ((336, 160, 160), (0, 0, 0, 0), (0, 0))
+QUANTS = ((512, 256, 256), (512, 512), (1024,))
 PIECES = ((0, 768), (768, 768), (1536, 512))
 ROWS = (4, 8, 0)
 LAST_PIECES = ((0, 768), (768, 768), (1536, 384), (1920, 128))
@@ -44,12 +42,14 @@ def tile_routed_moe_kernel(tc, xT, w_words, w_scales, b, gate, offs, pos1, pos2,
 
         raws = {}
         for a in range(PASSES):
-            for i, (t0, n, v) in enumerate(CHUNKS[a]):
+            t0 = 0
+            for i, n in enumerate(LOADS[a]):
                 raw = keep.tile([P, 4, n], F32, name=f"raw{a}_{i}")
-                raws[a, i] = raw
+                raws[a, t0] = raw
                 nc.sync.dma_start(raw[:], xT[512 * a : 512 * (a + 1), t0 : t0 + n].rearrange("(p t) n -> p t n", t=4))
-                if a == 0 and i == 0:
-                    nc.sync.dma_start(offs_t[:], offs)
+                t0 += n
+            if a == 0:
+                nc.sync.dma_start(offs_t[:], offs)
 
         wsc = keep.tile([P, E * PASSES * N // 4], I32, name="wsc", align_bytes=64)
         nc.vector.memset(wsc[:], 0)
@@ -98,33 +98,33 @@ def tile_routed_moe_kernel(tc, xT, w_words, w_scales, b, gate, offs, pos1, pos2,
         def gather(dst, src, lo, n):
             nc.vector.tensor_copy(dst[:, lo : lo + n], src[:].indirect(offs_t[:, lo // 16 : (lo + n) // 16]))
 
-        def cast(engine_copy, grouped, raw, lo, hi):
+        def cast(engine_copy, grouped, raw, t0, lo, hi):
             engine_copy(
-                grouped[:, 4 * lo : 4 * hi].rearrange("p (c i t) -> p c t i", i=4, t=4),
+                grouped[:, 4 * (t0 + lo) : 4 * (t0 + hi)].rearrange("p (c i t) -> p c t i", i=4, t=4),
                 raw[:, :, lo:hi].rearrange("p t (c i) -> p c t i", i=4),
             )
 
-        def quantise(a, t0, n, grouped):
-            nc.vector.quantize_mx(
-                out=words[a][:, t0 : t0 + n].bitcast(FP8X4),
-                scales=plane[ROWS[a] : P, t0 : t0 + n],
-                in_=grouped[:],
-            )
-
         for a in range(PASSES):
-            if a < PASSES - 1:
-                for i, (t0, n, v) in enumerate(CHUNKS[a]):
-                    grouped = keep.tile([P, 4 * n], BF16, name=f"grouped{a}_{i}", align_bytes=64)
-                    if v < n:
-                        cast(nc.scalar.copy, grouped[:], raws[a, i], v, n)
-                    if v > 0:
-                        cast(nc.vector.tensor_copy, grouped[:], raws[a, i], 0, v)
-                    quantise(a, t0, n, grouped)
-            else:
-                grouped = keep.tile([P, 4 * T], BF16, name="grouped_last", align_bytes=64)
-                for i, (t0, n, v) in enumerate(CHUNKS[a]):
-                    cast(nc.scalar.copy, grouped[:, 4 * t0 : 4 * (t0 + n)], raws[a, i], 0, n)
-                quantise(a, 0, T, grouped)
+            grouped = keep.tile([P, 4 * T], BF16, name=f"grouped{a}", align_bytes=64)
+            ends = []
+            t0 = 0
+            for m in QUANTS[a]:
+                ends.append((t0, m))
+                t0 += m
+            t0 = 0
+            for n, v in zip(LOADS[a], VECTOR_CASTS[a]):
+                if v < n:
+                    cast(nc.scalar.copy, grouped, raws[a, t0], t0, v, n)
+                if v > 0:
+                    cast(nc.vector.tensor_copy, grouped, raws[a, t0], t0, 0, v)
+                t0 += n
+                for q0, m in ends:
+                    if q0 + m == t0:
+                        nc.vector.quantize_mx(
+                            out=words[a][:, q0:t0].bitcast(FP8X4),
+                            scales=plane[ROWS[a] : P, q0:t0],
+                            in_=grouped[:, 4 * q0 : 4 * t0],
+                        )
             if a < PASSES - 1:
                 for lo, n in PIECES:
                     gather(gwords[a], words[a], lo, n)
@@ -152,7 +152,7 @@ def tile_routed_moe_kernel(tc, xT, w_words, w_scales, b, gate, offs, pos1, pos2,
 
         def open_group(g):
             e, s, m = g
-            acc = psum.tile([P, 512], F32, name=f"acc{groups.index(g) % 7}")
+            acc = psum.tile([P, 512], F32, name=f"acc{groups.index(g) % 6}")
             accs[s] = acc
             mm(acc[:, 0:m], e, s, m, range(last))
 
@@ -161,7 +161,7 @@ def tile_routed_moe_kernel(tc, xT, w_words, w_scales, b, gate, offs, pos1, pos2,
             mm(accs[s][:, 0:m], e, s, m, (last,))
             nc.scalar.activation(y[:, s : s + m], accs[s][:, 0:m], SILU, bias=bias[:, e : e + 1])
 
-        for g in groups[:7]:
+        for g in groups[:6]:
             open_group(g)
         for lo, n in LAST_PIECES:
             gather(gwords[last], words[last], lo, n)
@@ -169,22 +169,26 @@ def tile_routed_moe_kernel(tc, xT, w_words, w_scales, b, gate, offs, pos1, pos2,
                 if lo <= g[1] < lo + n:
                     close_group(g)
             if lo == 0:
-                for g in groups[7:]:
+                for g in groups[6:]:
                     open_group(g)
 
         m1 = keep.tile([P, T], F32, name="m1")
         m2 = keep.tile([P, T], F32, name="m2")
         res = keep.tile([P, T], F32, name="res")
         nc.vector.tensor_tensor(m1[:], y[:].indirect(pos1_t[:]), gates[0][:], MULT)
+        banks = ((0, 256), (256, 384))
         R = 384
+        totals = []
+        for lo, hi in banks:
+            total = psum.tile([P, 512], F32, name=f"total{lo}")
+            totals.append(total)
+            nc.tensor.matmul(total[:, 0 : hi - lo], ident[:], m1[:, lo:hi], start=True, stop=False)
         for lo, hi in ((0, R), (R, T)):
             nc.vector.tensor_tensor(m2[:, lo:hi], y[:].indirect(pos2_t[:, lo // 16 : hi // 16]), gates[1][:, lo:hi], MULT)
-            if lo == 0:
-                total = psum.tile([P, 512], F32, name="total")
-                nc.tensor.matmul(total[:, 0:R], ident[:], m1[:, 0:R], start=True, stop=False)
-                nc.tensor.matmul(total[:, 0:R], ident[:], m2[:, 0:R], start=False, stop=True)
-                nc.scalar.copy(res[:, 0:R], total[:, 0:R])
-                nc.sync.dma_start(out[:, 0:R], res[:, 0:R])
+        for (lo, hi), total in zip(banks, totals):
+            nc.tensor.matmul(total[:, 0 : hi - lo], ident[:], m2[:, lo:hi], start=False, stop=True)
+            nc.scalar.copy(res[:, lo:hi], total[:, 0 : hi - lo])
+        nc.sync.dma_start(out[:, 0:R], res[:, 0:R])
         for lo, hi in ((R, 768), (768, T)):
             nc.vector.tensor_tensor(res[:, lo:hi], m1[:, lo:hi], m2[:, lo:hi], ADD)
             nc.sync.dma_start(out[:, lo:hi], res[:, lo:hi])

@@ -22,7 +22,7 @@ PASSES = K // 512
 S = E * C
 
 LOADS = ((512, 256, 256), (256, 256, 256, 256), (512, 512))
-VECTOR_CASTS = ((336, 160, 160), (0, 0, 0, 0), (0, 0))
+VECTOR_CASTS = ((336, 192, 192), (0, 0, 0, 0), (0, 0))
 QUANTS = ((512, 256, 256), (512, 512), (1024,))
 PIECES = ((0, 768), (768, 768), (1536, 512))
 ROWS = (4, 8, 0)
@@ -183,7 +183,7 @@ def tile_routed_moe_kernel(tc, xT, w_words, w_scales, b, gate, offs, pos1, pos2,
             total = psum.tile([P, 512], F32, name=f"total{lo}")
             totals.append(total)
             nc.tensor.matmul(total[:, 0 : hi - lo], ident[:], m1[:, lo:hi], start=True, stop=False)
-        for lo, hi in ((0, R), (R, T)):
+        for lo, hi in ((0, R), (R, 768), (768, T)):
             nc.vector.tensor_tensor(m2[:, lo:hi], y[:].indirect(pos2_t[:, lo // 16 : hi // 16]), gates[1][:, lo:hi], MULT)
         for (lo, hi), total in zip(banks, totals):
             nc.tensor.matmul(total[:, 0 : hi - lo], ident[:], m2[:, lo:hi], start=False, stop=True)

from contextlib import ExitStack

import concourse.mybir as mybir
from concourse.masks import make_identity

K, T, E, C, N = 1536, 1024, 8, 256, 128
FLOPS = 2 * K * E * C * N

F32 = mybir.dt.float32
BF16 = mybir.dt.bfloat16
I32 = mybir.dt.int32
U32 = mybir.dt.uint32
U16 = mybir.dt.uint16
U8 = mybir.dt.uint8
FP8X4 = mybir.dt.float8_e4m3fn_x4
MULT = mybir.AluOpType.mult
ADD = mybir.AluOpType.add
SILU = mybir.ActivationFunctionType.Silu

P = 128
PASSES = K // 512
S = E * C

LOADS = ((512, 256, 256), (256, 256, 256, 256), (512, 512))
VECTOR_CASTS = ((336, 192, 192), (0, 0, 0, 0), (0, 0))
QUANTS = ((512, 256, 256), (512, 512), (1024,))
PIECES = ((0, 768), (768, 768), (1536, 512))
ROWS = (4, 8, 0)
LAST_PIECES = ((0, 768), (768, 768), (1536, 384), (1920, 128))


def tile_routed_moe_kernel(tc, xT, w_words, w_scales, b, gate, offs, pos1, pos2, out):
    nc = tc.nc
    with ExitStack() as ctx:
        lists = ctx.enter_context(tc.tile_pool(name="lists", bufs=1))
        keep = ctx.enter_context(tc.tile_pool(name="keep", bufs=1))
        psum = ctx.enter_context(tc.psum_pool(name="psum", bufs=1))

        offs_t = lists.tile([P, S // 16], U16, name="offs_t")
        pos1_t = lists.tile([P, T // 16], U16, name="pos1_t")
        pos2_t = lists.tile([P, T // 16], U16, name="pos2_t")

        raws = {}
        for a in range(PASSES):
            t0 = 0
            for i, n in enumerate(LOADS[a]):
                raw = keep.tile([P, 4, n], F32, name=f"raw{a}_{i}")
                raws[a, t0] = raw
                nc.sync.dma_start(raw[:], xT[512 * a : 512 * (a + 1), t0 : t0 + n].rearrange("(p t) n -> p t n", t=4))
                t0 += n
            if a == 0:
                nc.sync.dma_start(offs_t[:], offs)

        wsc = keep.tile([P, E * PASSES * N // 4], I32, name="wsc", align_bytes=64)
        nc.vector.memset(wsc[:], 0)
        plane = keep.tile([P, T], U8, name="plane", align_bytes=64)
        nc.gpsimd.memset(plane[:], 0)
        ident = keep.tile([P, P], F32, name="ident")
        make_identity(nc, ident[:])
        one = keep.tile([P, 1], F32, name="one")
        nc.vector.memset(one[:], 0.0)
        warm = keep.tile([P, 1], F32, name="warm")
        nc.scalar.activation(warm[:], one[:], SILU)

        w = keep.tile([P, E * PASSES * N], I32, name="w", align_bytes=64)
        w_hbm = w_words.rearrange("e a p n r -> e a p (n r)").bitcast(I32).rearrange("e a p n -> p (e a) n")
        half = E * PASSES // 2
        for h in range(2):
            nc.sync.dma_start(
                w[:, h * half * N : (h + 1) * half * N].rearrange("p (g n) -> p g n", n=N),
                w_hbm[:, h * half : (h + 1) * half, :],
            )
        for q in range(4):
            nc.sync.dma_start(
                wsc[32 * q : 32 * q + 4, :].rearrange("r (g n) -> r g n", n=N // 4),
                w_scales.bitcast(I32)[:, :, 4 * q : 4 * q + 4, :].rearrange("e a r n -> r (e a) n"),
            )
        bias = keep.tile([P, E], F32, name="bias")
        nc.sync.dma_start(bias[:], b)
        nc.sync.dma_start(pos1_t[:], pos1)
        gates = []
        for r in range(2):
            g = keep.tile([P, T], F32, name=f"gate{r}")
            gates.append(g)
            nc.sync.dma_start(g[:], gate[r])
            if r == 0:
                nc.sync.dma_start(pos2_t[:], pos2)

        gbytes = keep.tile([P, S], U8, name="gbytes", align_bytes=64)
        words = []
        gwords = []
        for a in range(PASSES):
            wt = keep.tile([P, T], U32, name=f"words{a}", align_bytes=64)
            words.append(wt)
            gt = keep.tile([P, S], U32, name=f"gwords{a}", align_bytes=64)
            gwords.append(gt)

        def gather(dst, src, lo, n):
            nc.vector.tensor_copy(dst[:, lo : lo + n], src[:].indirect(offs_t[:, lo // 16 : (lo + n) // 16]))

        def cast(engine_copy, grouped, raw, t0, lo, hi):
            engine_copy(
                grouped[:, 4 * (t0 + lo) : 4 * (t0 + hi)].rearrange("p (c i t) -> p c t i", i=4, t=4),
                raw[:, :, lo:hi].rearrange("p t (c i) -> p c t i", i=4),
            )

        for a in range(PASSES):
            grouped = keep.tile([P, 4 * T], BF16, name=f"grouped{a}", align_bytes=64)
            ends = []
            t0 = 0
            for m in QUANTS[a]:
                ends.append((t0, m))
                t0 += m
            t0 = 0
            for n, v in zip(LOADS[a], VECTOR_CASTS[a]):
                if v < n:
                    cast(nc.scalar.copy, grouped, raws[a, t0], t0, v, n)
                if v > 0:
                    cast(nc.vector.tensor_copy, grouped, raws[a, t0], t0, 0, v)
                t0 += n
                for q0, m in ends:
                    if q0 + m == t0:
                        nc.vector.quantize_mx(
                            out=words[a][:, q0:t0].bitcast(FP8X4),
                            scales=plane[ROWS[a] : P, q0:t0],
                            in_=grouped[:, 4 * q0 : 4 * t0],
                        )
            if a < PASSES - 1:
                for lo, n in PIECES:
                    gather(gwords[a], words[a], lo, n)
        for lo, n in PIECES:
            gather(gbytes, plane, lo, n)

        y = keep.tile([P, S], F32, name="y")

        def mm(acc, e, lo, n, passes):
            for a in passes:
                g = e * PASSES + a
                nc.tensor.matmul_mx(
                    out=acc,
                    lhsT=w[:, g * N : (g + 1) * N].bitcast(FP8X4),
                    lhsT_scale=wsc[:, g * N // 4 : (g + 1) * N // 4].bitcast(U8),
                    rhs=gwords[a][:, lo : lo + n].bitcast(FP8X4),
                    rhs_scale=gbytes[ROWS[a] : P, lo : lo + n],
                    start=(a == 0),
                    stop=(a == PASSES - 1),
                )

        groups = [(e, C * e, C) for e in range(E - 1)] + [(E - 1, S - C, N), (E - 1, S - N, N)]
        accs = {}
        last = PASSES - 1

        def open_group(g):
            e, s, m = g
            acc = psum.tile([P, 512], F32, name=f"acc{groups.index(g) % 6}")
            accs[s] = acc
            mm(acc[:, 0:m], e, s, m, range(last))

        def close_group(g):
            e, s, m = g
            mm(accs[s][:, 0:m], e, s, m, (last,))
            nc.scalar.activation(y[:, s : s + m], accs[s][:, 0:m], SILU, bias=bias[:, e : e + 1])

        for g in groups[:6]:
            open_group(g)
        for lo, n in LAST_PIECES:
            gather(gwords[last], words[last], lo, n)
            for g in groups:
                if lo <= g[1] < lo + n:
                    close_group(g)
            if lo == 0:
                for g in groups[6:]:
                    open_group(g)

        m1 = keep.tile([P, T], F32, name="m1")
        m2 = keep.tile([P, T], F32, name="m2")
        res = keep.tile([P, T], F32, name="res")
        nc.vector.tensor_tensor(m1[:], y[:].indirect(pos1_t[:]), gates[0][:], MULT)
        banks = ((0, 256), (256, 384))
        R = 384
        totals = []
        for lo, hi in banks:
            total = psum.tile([P, 512], F32, name=f"total{lo}")
            totals.append(total)
            nc.tensor.matmul(total[:, 0 : hi - lo], ident[:], m1[:, lo:hi], start=True, stop=False)
        for lo, hi in ((0, R), (R, 768), (768, T)):
            nc.vector.tensor_tensor(m2[:, lo:hi], y[:].indirect(pos2_t[:, lo // 16 : hi // 16]), gates[1][:, lo:hi], MULT)
        for (lo, hi), total in zip(banks, totals):
            nc.tensor.matmul(total[:, 0 : hi - lo], ident[:], m2[:, lo:hi], start=False, stop=True)
            nc.scalar.copy(res[:, lo:hi], total[:, 0 : hi - lo])
        nc.sync.dma_start(out[:, 0:R], res[:, 0:R])
        for lo, hi in ((R, 768), (768, T)):
            nc.vector.tensor_tensor(res[:, lo:hi], m1[:, lo:hi], m2[:, lo:hi], ADD)
            nc.sync.dma_start(out[:, lo:hi], res[:, lo:hi])
